import numpy as np
import ml_dtypes


def mxq(x, axis, fmt="e4m3"):
    dtype, down = {"e4m3": (ml_dtypes.float8_e4m3fn, 7), "e5m2": (ml_dtypes.float8_e5m2, 14)}[fmt]
    v = np.moveaxis(np.asarray(x, np.float32).astype(ml_dtypes.bfloat16).astype(np.float64), axis, -1)
    blocks = v.reshape(v.shape[:-1] + (-1, 32))
    amax = np.abs(blocks).max(-1, keepdims=True)
    byte = np.maximum(np.where(amax > 0, np.frexp(amax)[1] - 1 + 127, 0) - down, 1)
    scale = np.exp2(byte - 127.0)
    codes = (blocks / scale).astype(np.float32).astype(dtype).astype(np.float64)
    return np.moveaxis((codes * scale).reshape(v.shape), -1, axis)


WIDE = False


def mx_kscale(k):
    if not WIDE:
        return np.ones(k)
    levels = np.array([30, -30])
    if k % 512:
        return np.exp2(np.random.permutation(np.resize(levels, k // 32))).repeat(32)
    a = np.empty((k // 512, 16))
    for p in range(k // 512):
        a[p, :8] = np.random.permutation(np.resize(levels, 8))
        for g in range(8):
            far = levels[np.abs(levels - a[p, g]) >= 10]
            a[p, g + 8] = far[np.random.randint(len(far))]
    return np.exp2(a.ravel()).repeat(32)


def f64(x):
    return np.asarray(x).astype(np.float64)


def striped(idx):
    return np.tile(np.asarray(idx).reshape(-1, 16).T, (8, 1)).astype(np.uint16)


def unstriped(offs):
    return offs[:16].T.reshape(-1).astype(np.int64)


E2M1 = np.array([0.0, 0.5, 1.0, 1.5, 2.0, 3.0, 4.0, 6.0, -0.0, -0.5, -1.0, -1.5, -2.0, -3.0, -4.0, -6.0])


def pack_weight(w, fmt):
    k, n = w.shape
    w = f64(np.asarray(w, np.float32).astype(ml_dtypes.bfloat16)).reshape(k // 32, 32, n)
    amax = np.abs(w).max(1)
    if fmt in ("e4m3", "e5m2"):
        byte = np.frexp(amax)[1] - 1 + 127 - (7 if fmt == "e4m3" else 14)
    else:
        mant, ex = np.frexp(amax / 6.0)
        byte = np.where(mant > 0.5, ex, ex - 1) + 127
    byte = np.clip(np.where(amax > 0, byte, 1), 1, 254)
    scaled = (w * np.exp2(127.0 - byte)[:, None, :]).reshape(k, n).astype(np.float32)
    by_word = np.ascontiguousarray(scaled.reshape(k // 512, 128, 4, n).transpose(0, 1, 3, 2))
    if fmt in ("e4m3", "e5m2"):
        words = by_word.astype(ml_dtypes.float8_e4m3fn if fmt == "e4m3" else ml_dtypes.float8_e5m2).view(np.uint8)
    else:
        c = by_word.astype(ml_dtypes.float4_e2m1fn).view(np.uint8) & 0xF
        words = (c[..., 0::2] | (c[..., 1::2] << 4)).reshape(k // 512, 128, 2 * n)
    return np.ascontiguousarray(words), np.ascontiguousarray(byte.astype(np.uint8).reshape(k // 512, 16, n))


def unpack_weight(words, scales, fmt):
    g, _, n = scales.shape
    words = np.ascontiguousarray(words).reshape(g, 128, n, -1)
    if fmt in ("e4m3", "e5m2"):
        vals = words.view(ml_dtypes.float8_e4m3fn if fmt == "e4m3" else ml_dtypes.float8_e5m2).astype(np.float64)
    else:
        nib = np.empty((g, 128, n, 4), np.uint8)
        nib[..., 0::2] = words & 0xF
        nib[..., 1::2] = words >> 4
        vals = E2M1[nib]
    vals = vals * np.repeat(np.exp2(scales.astype(np.float64) - 127.0), 8, axis=1)[..., None]
    return vals.transpose(0, 1, 3, 2).reshape(g * 512, n)


K, T, J, R, C, O, N, E = 512, 1024, 256, 512, 512, 256, 256, 1024


def setup_inputs():
    n = np.random.standard_normal
    idx = np.random.permutation(T)[:J]
    idx2 = np.random.permutation(C)[:J]
    idx3 = np.random.permutation(C)[:J]
    idx4 = np.random.permutation(C)[:O]
    idx5 = np.random.permutation(T)[:O]
    idx6 = np.random.permutation(E)[:O]
    fk = mx_kscale(K)
    fr = mx_kscale(R)
    xtp = pack_weight(n((K, T)) / fk[:, None], "e2m1")
    wp = pack_weight(n((K, R)) * 1 / np.sqrt(K) * fk[:, None] * fr, "e5m2")
    wbp = pack_weight(n((R, N)) * 1 / np.sqrt(R) / fr[:, None], "e4m3")
    wsp = pack_weight(n((K, N)) * 1 / np.sqrt(K) * fk[:, None], "e4m3")
    return {
        "xt_words": xtp[0],
        "xt_scales": xtp[1],
        "w_words": wp[0],
        "w_scales": wp[1],
        "wb_words": wbp[0],
        "wb_scales": wbp[1],
        "ws_words": wsp[0],
        "ws_scales": wsp[1],
        "tz": (n((N, E))).astype(np.float32),
        "offs": striped(idx),
        "offs2": striped(idx2),
        "offs3": striped(idx3),
        "offs4": striped(idx4),
        "offs5": striped(idx5),
        "offs6": striped(idx6),
    }


def reference(xt_words, xt_scales, w_words, w_scales, wb_words, wb_scales, ws_words, ws_scales, tz, offs, offs2, offs3, offs4, offs5, offs6):
    idx = unstriped(offs)
    idx2 = unstriped(offs2)
    idx3 = unstriped(offs3)
    idx4 = unstriped(offs4)
    idx5 = unstriped(offs5)
    idx6 = unstriped(offs6)
    xtu = unpack_weight(xt_words, xt_scales, "e2m1")
    wu = unpack_weight(w_words, w_scales, "e5m2")
    wbu = unpack_weight(wb_words, wb_scales, "e4m3")
    wsu = unpack_weight(ws_words, ws_scales, "e4m3")
    xtidxg = xtu[:, idx]
    a = wu.T @ xtidxg
    pw = np.zeros((R, C))
    pw[:, idx2] = a
    pv = np.zeros((R, C))
    pv[:, idx3] = a
    pg = pw + pv
    hid = np.maximum(pg[:, idx4], 0.0)
    hidq = mxq(hid, 0, "e5m2")
    xtidx5g = xtu[:, idx5]
    p = wbu.T @ hidq + wsu.T @ xtidx5g
    y = p + f64(tz)[:, idx6]
    return y

@@ -1,0 +1,202 @@
+from contextlib import ExitStack
+
+import concourse.mybir as mybir
+
+K, T, J, R, C, O, N, E = 512, 1024, 256, 512, 512, 256, 256, 1024
+FLOPS = 2 * K * R * J + 2 * R * N * O + 2 * K * N * O
+
+F32 = mybir.dt.float32
+BF16 = mybir.dt.bfloat16
+I32 = mybir.dt.int32
+U32 = mybir.dt.uint32
+U16 = mybir.dt.uint16
+U8 = mybir.dt.uint8
+E4M3 = mybir.dt.float8_e4m3fn_x4
+E5M2 = mybir.dt.float8_e5m2_x4
+E2M1 = mybir.dt.float4_e2m1fn_x4
+ALU = mybir.AluOpType
+ACT = mybir.ActivationFunctionType
+
+P = 128
+PACK = 4
+QUADS = 4
+BOARDS = 2
+ROUND_ON_VECTOR = 160
+
+
+def tile_list_postedtwice_solo_further_tabled_kernel(
+    tc, xt_words, xt_scales, w_words, w_scales, wb_words, wb_scales, ws_words, ws_scales,
+    tz, offs, offs2, offs3, offs4, offs5, offs6, out,
+):
+    nc = tc.nc
+
+    with ExitStack() as ctx:
+        keep = ctx.enter_context(tc.tile_pool(name="keep", bufs=1))
+        psum = ctx.enter_context(tc.psum_pool(name="psum", bufs=1))
+
+        def sbuf(name, width, dtype):
+            return keep.tile([P, width], dtype, name=name, align_bytes=64)
+
+        def load_list(name, src):
+            lst = keep.tile([P, J // 16], U16, name=name)
+            nc.sync.dma_start(lst[:], src)
+            return lst
+
+        def load_scale_rows(queue, plane, src):
+            for q in range(QUADS):
+                queue.dma_start(
+                    plane[32 * q : 32 * q + 4, :].bitcast(I32),
+                    src[0, 4 * q : 4 * q + 4, :].bitcast(I32),
+                )
+
+        def word_rows(src):
+            return src[0].rearrange("p n b -> p (n b)").bitcast(I32)
+
+        xt_s = sbuf("xt_s", T, U8)
+        w_s = sbuf("w_s", R, U8)
+        wb_s = sbuf("wb_s", N, U8)
+        ws_s = sbuf("ws_s", N, U8)
+        nc.vector.memset(xt_s[:].bitcast(I32), 0)
+        nc.gpsimd.memset(w_s[:].bitcast(I32), 0)
+
+        xt_w = sbuf("xt_w", T, U16)
+        w_w = sbuf("w_w", R, U32)
+        slots = load_list("slots", offs)
+        nc.sync.dma_start(xt_w[:].bitcast(I32), xt_words[0].bitcast(I32))
+        nc.sync.dma_start(w_w[:].bitcast(I32), word_rows(w_words))
+        load_scale_rows(nc.sync, xt_s, xt_scales)
+        load_scale_rows(nc.sync, w_s, w_scales)
+        posts_w = load_list("posts_w", offs2)
+        posts_v = load_list("posts_v", offs3)
+        shorts = load_list("shorts", offs5)
+        reads = load_list("reads", offs4)
+        entries = load_list("entries", offs6)
+
+        pw = [sbuf("pw%d" % b, C, F32) for b in range(BOARDS)]
+        pv = [sbuf("pv%d" % b, C, F32) for b in range(BOARDS)]
+        for b in range(BOARDS):
+            nc.vector.memset(pw[b][:], 0.0)
+            nc.vector.memset(pv[b][:], 0.0)
+        for plane in (ws_s, wb_s):
+            nc.vector.memset(plane[:].bitcast(I32), 0)
+
+        ws_w = sbuf("ws_w", N, U32)
+        wb_w = sbuf("wb_w", N, U32)
+        tz_rows = [sbuf("tz_rows%d" % h, E, F32) for h in range(N // P)]
+        load_scale_rows(nc.sync, ws_s, ws_scales)
+        load_scale_rows(nc.sync, wb_s, wb_scales)
+        nc.sync.dma_start(ws_w[:].bitcast(I32), word_rows(ws_words))
+        nc.sync.dma_start(wb_w[:].bitcast(I32), word_rows(wb_words))
+        for h in range(N // P):
+            nc.sync.dma_start(tz_rows[h][:], tz[h * P : (h + 1) * P, :])
+
+        xg_w = sbuf("xg_w", J, U16)
+        xg_s = sbuf("xg_s", J, U8)
+        nc.vector.tensor_copy(xg_w[:], xt_w[:].indirect(slots[:]))
+        nc.vector.tensor_copy(xg_s[:], xt_s[:].indirect(slots[:]))
+
+        wd_w = sbuf("wd_w", R, U32)
+        wd_s = sbuf("wd_s", R, U8)
+        nc.scalar.copy(
+            wd_w[:].rearrange("p (t m) -> p t m", t=PACK),
+            w_w[:].rearrange("p (m t) -> p t m", t=PACK),
+        )
+        nc.vector.tensor_copy(
+            wd_s[:].rearrange("p (t m) -> p t m", t=PACK),
+            w_s[:].rearrange("p (m t) -> p t m", t=PACK),
+        )
+
+        a_ps = [psum.tile([P, J], F32, name="a_ps%d" % t) for t in range(PACK)]
+        for t in range(PACK):
+            cols = slice(t * P, (t + 1) * P)
+            nc.tensor.matmul_mx(
+                out=a_ps[t][:],
+                lhsT=wd_w[:, cols].bitcast(E5M2), lhsT_scale=wd_s[:, cols],
+                rhs=xg_w[:].bitcast(E2M1), rhs_scale=xg_s[:],
+                start=True, stop=True,
+            )
+
+        xs_w = sbuf("xs_w", O, U16)
+        xs_s = sbuf("xs_s", O, U8)
+        nc.vector.tensor_copy(xs_w[:], xt_w[:].indirect(shorts[:]))
+
+        a = [sbuf("a%d" % t, J, F32) for t in range(PACK)]
+        pg = [sbuf("pg%d" % t, C, F32) for t in range(PACK)]
+        picked = keep.tile([P, PACK, O], F32, name="picked", align_bytes=64)
+
+        def post(t):
+            nc.vector.tensor_copy(pw[t % BOARDS][:].indirect(posts_w[:]), a[t][:])
+            nc.scalar.activation(pv[t % BOARDS][:].indirect(posts_v[:]), a[t][:], ACT.Copy)
+
+        def join(t):
+            nc.vector.tensor_tensor(pg[t][:], pw[t % BOARDS][:], pv[t % BOARDS][:], ALU.add)
+
+        def read(t):
+            nc.scalar.activation(picked[:, t, :], pg[t][:].indirect(reads[:]), ACT.Copy)
+
+        nc.scalar.copy(a[0][:], a_ps[0][:])
+        nc.vector.tensor_copy(a[1][:], a_ps[1][:])
+        post(0)
+        nc.scalar.copy(a[2][:], a_ps[2][:])
+        nc.scalar.copy(a[3][:], a_ps[3][:])
+        post(1)
+        join(0)
+        nc.vector.tensor_copy(xs_s[:], xt_s[:].indirect(shorts[:]))
+        post(2)
+        read(0)
+        join(1)
+        join(2)
+        post(3)
+        read(1)
+        read(2)
+        join(3)
+
+        p_ps = [psum.tile([P, O], F32, name="p_ps%d" % h) for h in range(N // P)]
+        for h in range(N // P):
+            cols = slice(h * P, (h + 1) * P)
+            nc.tensor.matmul_mx(
+                out=p_ps[h][:],
+                lhsT=ws_w[:, cols].bitcast(E4M3), lhsT_scale=ws_s[:, cols],
+                rhs=xs_w[:].bitcast(E2M1), rhs_scale=xs_s[:],
+                start=True, stop=False,
+            )
+
+        last = PACK - 1
+        half = O // 2
+        nc.vector.tensor_copy(picked[:, last, :half], pg[last][:].indirect(reads[:, : half // 16]))
+        nc.scalar.activation(picked[:, last, half:], pg[last][:].indirect(reads[:, half // 16 :]), ACT.Copy)
+
+        hid = keep.tile([P, O, PACK], BF16, name="hid", align_bytes=64)
+
+        def woven(lo, hi):
+            dst = hid[:, lo:hi, :].rearrange("p (c i) t -> p c t i", i=4)
+            src = picked[:, :, lo:hi].rearrange("p t (c i) -> p c t i", i=4)
+            return dst, src
+
+        dst, src = woven(0, ROUND_ON_VECTOR)
+        nc.vector.tensor_scalar_max(dst, src, 0.0)
+        dst, src = woven(ROUND_ON_VECTOR, O)
+        nc.scalar.activation(dst, src, ACT.Relu)
+
+        hq_w = sbuf("hq_w", O, U32)
+        hq_s = sbuf("hq_s", O, U8)
+        nc.vector.quantize_mx(
+            out=hq_w[:].bitcast(E5M2), scales=hq_s[:],
+            in_=hid[:].rearrange("p o t -> p (o t)"),
+        )
+
+        tz_picked = [sbuf("tz_picked%d" % h, O, F32) for h in range(N // P)]
+        for h in range(N // P):
+            nc.scalar.activation(tz_picked[h][:], tz_rows[h][:].indirect(entries[:]), ACT.Copy)
+
+        for h, queue in enumerate((nc.sync, nc.scalar)):
+            cols = slice(h * P, (h + 1) * P)
+            nc.tensor.matmul_mx(
+                out=p_ps[h][:],
+                lhsT=wb_w[:, cols].bitcast(E4M3), lhsT_scale=wb_s[:, cols],
+                rhs=hq_w[:].bitcast(E5M2), rhs_scale=hq_s[:],
+                start=False, stop=True,
+            )
+            y = sbuf("y%d" % h, O, F32)
+            nc.vector.tensor_tensor(y[:], p_ps[h][:], tz_picked[h][:], ALU.add)
+            queue.dma_start(out[cols, :], y[:])

@@ -20,8 +20,7 @@ ACT = mybir.ActivationFunctionType
 P = 128
 PACK = 4
 QUADS = 4
-BOARDS = 2
-ROUND_ON_VECTOR = 160
+BOARDS = 3
 
 
 def tile_list_postedtwice_solo_further_tabled_kernel(
@@ -34,8 +33,8 @@ def tile_list_postedtwice_solo_further_tabled_kernel(
         keep = ctx.enter_context(tc.tile_pool(name="keep", bufs=1))
         psum = ctx.enter_context(tc.psum_pool(name="psum", bufs=1))
 
-        def sbuf(name, width, dtype):
-            return keep.tile([P, width], dtype, name=name, align_bytes=64)
+        def sbuf(name, width, dtype, tag=None):
+            return keep.tile([P, width], dtype, name=name, tag=tag or name, align_bytes=64)
 
         def load_list(name, src):
             lst = keep.tile([P, J // 16], U16, name=name)
@@ -56,29 +55,30 @@ def tile_list_postedtwice_solo_further_tabled_kernel(
         w_s = sbuf("w_s", R, U8)
         wb_s = sbuf("wb_s", N, U8)
         ws_s = sbuf("ws_s", N, U8)
-        nc.vector.memset(xt_s[:].bitcast(I32), 0)
-        nc.gpsimd.memset(w_s[:].bitcast(I32), 0)
+        xt_s_landed = sbuf("xt_s_landed", T, U8)
+        for plane in (w_s, xt_s):
+            nc.vector.memset(plane[:].bitcast(I32), 0)
 
         xt_w = sbuf("xt_w", T, U16)
         w_w = sbuf("w_w", R, U32)
         slots = load_list("slots", offs)
+        load_scale_rows(nc.sync, xt_s_landed, xt_scales)
         nc.sync.dma_start(xt_w[:].bitcast(I32), xt_words[0].bitcast(I32))
         nc.sync.dma_start(w_w[:].bitcast(I32), word_rows(w_words))
-        load_scale_rows(nc.sync, xt_s, xt_scales)
         load_scale_rows(nc.sync, w_s, w_scales)
-        posts_w = load_list("posts_w", offs2)
-        posts_v = load_list("posts_v", offs3)
         shorts = load_list("shorts", offs5)
+        posts_v = load_list("posts_v", offs3)
+        posts_w = load_list("posts_w", offs2)
         reads = load_list("reads", offs4)
         entries = load_list("entries", offs6)
 
-        pw = [sbuf("pw%d" % b, C, F32) for b in range(BOARDS)]
-        pv = [sbuf("pv%d" % b, C, F32) for b in range(BOARDS)]
-        for b in range(BOARDS):
-            nc.vector.memset(pw[b][:], 0.0)
-            nc.vector.memset(pv[b][:], 0.0)
+        pw = [sbuf("pw%d" % b, C, F32) for b in range(BOARDS - 1)]
+        pv = [sbuf("pv%d" % b, C, F32) for b in range(BOARDS - 1)]
+        for b, engine in enumerate((nc.vector, nc.gpsimd)):
+            engine.memset(pv[b][:], 0.0)
+            engine.memset(pw[b][:], 0.0)
         for plane in (ws_s, wb_s):
-            nc.vector.memset(plane[:].bitcast(I32), 0)
+            nc.gpsimd.memset(plane[:].bitcast(I32), 0)
 
         ws_w = sbuf("ws_w", N, U32)
         wb_w = sbuf("wb_w", N, U32)
@@ -90,113 +90,134 @@ def tile_list_postedtwice_solo_further_tabled_kernel(
         for h in range(N // P):
             nc.sync.dma_start(tz_rows[h][:], tz[h * P : (h + 1) * P, :])
 
+        for q in range(QUADS):
+            live = slice(32 * q, 32 * q + 4)
+            nc.vector.tensor_copy(xt_s[live, :].bitcast(I32), xt_s_landed[live, :].bitcast(I32))
+
         xg_w = sbuf("xg_w", J, U16)
         xg_s = sbuf("xg_s", J, U8)
         nc.vector.tensor_copy(xg_w[:], xt_w[:].indirect(slots[:]))
         nc.vector.tensor_copy(xg_s[:], xt_s[:].indirect(slots[:]))
 
         wd_w = sbuf("wd_w", R, U32)
-        wd_s = sbuf("wd_s", R, U8)
         nc.scalar.copy(
-            wd_w[:].rearrange("p (t m) -> p t m", t=PACK),
-            w_w[:].rearrange("p (m t) -> p t m", t=PACK),
+            wd_w[:].rearrange("p (t m) -> p m t", t=PACK),
+            w_w[:].rearrange("p (m t) -> p m t", t=PACK),
         )
+        w_s_dealt = w_s[:].rearrange("p (m t) -> p t m", t=PACK)
+        wd_s_first = sbuf("wd_s_first", P, U8)
+        wd_s_rest = sbuf("wd_s_rest", R - P, U8)
+        nc.vector.tensor_copy(wd_s_first[:], w_s_dealt[:, 0, :])
         nc.vector.tensor_copy(
-            wd_s[:].rearrange("p (t m) -> p t m", t=PACK),
-            w_s[:].rearrange("p (m t) -> p t m", t=PACK),
+            wd_s_rest[:].rearrange("p (t m) -> p t m", m=P), w_s_dealt[:, 1:, :]
         )
+        wd_s = [wd_s_first[:]] + [wd_s_rest[:, t * P : (t + 1) * P] for t in range(PACK - 1)]
 
-        a_ps = [psum.tile([P, J], F32, name="a_ps%d" % t) for t in range(PACK)]
+        xs_w = sbuf("xs_w", O, U16)
+        xs_s = sbuf("xs_s", O, U8)
+
+        a_ps0 = psum.tile([P, J], F32, name="a_ps0")
+        a_ps1 = psum.tile([P, J], F32, name="a_ps1")
+        a_ps23 = psum.tile([P, 2 * J], F32, name="a_ps23")
+        a_ps = [a_ps0[:], a_ps1[:], a_ps23[:, :J], a_ps23[:, J:]]
         for t in range(PACK):
-            cols = slice(t * P, (t + 1) * P)
             nc.tensor.matmul_mx(
-                out=a_ps[t][:],
-                lhsT=wd_w[:, cols].bitcast(E5M2), lhsT_scale=wd_s[:, cols],
+                out=a_ps[t],
+                lhsT=wd_w[:, t * P : (t + 1) * P].bitcast(E5M2), lhsT_scale=wd_s[t],
                 rhs=xg_w[:].bitcast(E2M1), rhs_scale=xg_s[:],
                 start=True, stop=True,
             )
 
-        xs_w = sbuf("xs_w", O, U16)
-        xs_s = sbuf("xs_s", O, U8)
-        nc.vector.tensor_copy(xs_w[:], xt_w[:].indirect(shorts[:]))
+        pv.append(sbuf("pv2", C, F32, tag="wd_w"))
+        pw.append(sbuf("pw2", C, F32, tag="xg_w"))
+        nc.gpsimd.memset(pv[2][:], 0.0)
+        nc.gpsimd.memset(pw[2][:], 0.0)
 
-        a = [sbuf("a%d" % t, J, F32) for t in range(PACK)]
+        a0 = sbuf("a0", J, F32)
+        a1 = sbuf("a1", J, F32)
+        a23 = sbuf("a23", 2 * J, F32)
+        a = [a0[:], a1[:], a23[:, :J], a23[:, J:]]
         pg = [sbuf("pg%d" % t, C, F32) for t in range(PACK)]
         picked = keep.tile([P, PACK, O], F32, name="picked", align_bytes=64)
 
         def post(t):
-            nc.vector.tensor_copy(pw[t % BOARDS][:].indirect(posts_w[:]), a[t][:])
-            nc.scalar.activation(pv[t % BOARDS][:].indirect(posts_v[:]), a[t][:], ACT.Copy)
+            nc.vector.tensor_copy(pw[t % BOARDS][:].indirect(posts_w[:]), a[t])
+            nc.scalar.activation(pv[t % BOARDS][:].indirect(posts_v[:]), a[t], ACT.Copy)
 
-        def join(t):
-            nc.vector.tensor_tensor(pg[t][:], pw[t % BOARDS][:], pv[t % BOARDS][:], ALU.add)
+        def join(t, engine):
+            engine.tensor_tensor(pg[t][:], pw[t % BOARDS][:], pv[t % BOARDS][:], ALU.add)
 
         def read(t):
             nc.scalar.activation(picked[:, t, :], pg[t][:].indirect(reads[:]), ACT.Copy)
 
-        nc.scalar.copy(a[0][:], a_ps[0][:])
-        nc.vector.tensor_copy(a[1][:], a_ps[1][:])
+        nc.scalar.copy(a0[:], a_ps0[:])
+        nc.scalar.copy(a1[:], a_ps1[:])
         post(0)
-        nc.scalar.copy(a[2][:], a_ps[2][:])
-        nc.scalar.copy(a[3][:], a_ps[3][:])
+        nc.scalar.copy(a23[:], a_ps23[:])
         post(1)
-        join(0)
+        join(0, nc.gpsimd)
+        nc.vector.tensor_copy(xs_w[:], xt_w[:].indirect(shorts[:]))
         nc.vector.tensor_copy(xs_s[:], xt_s[:].indirect(shorts[:]))
         post(2)
-        read(0)
-        join(1)
-        join(2)
+        join(1, nc.gpsimd)
         post(3)
+        join(2, nc.gpsimd)
+        nc.vector.tensor_copy(picked[:, 0, :], pg[0][:].indirect(reads[:]))
         read(1)
         read(2)
-        join(3)
+        join(3, nc.vector)
 
-        p_ps = [psum.tile([P, O], F32, name="p_ps%d" % h) for h in range(N // P)]
-        for h in range(N // P):
-            cols = slice(h * P, (h + 1) * P)
-            nc.tensor.matmul_mx(
-                out=p_ps[h][:],
-                lhsT=ws_w[:, cols].bitcast(E4M3), lhsT_scale=ws_s[:, cols],
-                rhs=xs_w[:].bitcast(E2M1), rhs_scale=xs_s[:],
-                start=True, stop=False,
-            )
+        halves = [slice(g * P, (g + 1) * P) for g in range(O // P)]
+        p_ps = [psum.tile([P, N // P, P], F32, name="p_ps%d" % g) for g in range(O // P)]
+        for g, reads_g in enumerate(halves):
+            for h in range(N // P):
+                cols = slice(h * P, (h + 1) * P)
+                nc.tensor.matmul_mx(
+                    out=p_ps[g][:, h, :],
+                    lhsT=ws_w[:, cols].bitcast(E4M3), lhsT_scale=ws_s[:, cols],
+                    rhs=xs_w[:, reads_g].bitcast(E2M1), rhs_scale=xs_s[:, reads_g],
+                    start=(h == 0), stop=False,
+                )
 
         last = PACK - 1
-        half = O // 2
-        nc.vector.tensor_copy(picked[:, last, :half], pg[last][:].indirect(reads[:, : half // 16]))
-        nc.scalar.activation(picked[:, last, half:], pg[last][:].indirect(reads[:, half // 16 :]), ACT.Copy)
+        nc.vector.tensor_copy(picked[:, last, halves[0]], pg[last][:].indirect(reads[:, : P // 16]))
+        nc.scalar.activation(picked[:, last, halves[1]], pg[last][:].indirect(reads[:, P // 16 :]), ACT.Copy)
 
-        hid = keep.tile([P, O, PACK], BF16, name="hid", align_bytes=64)
+        hid = [keep.tile([P, P, PACK], BF16, name="hid%d" % g, align_bytes=64) for g in range(O // P)]
 
-        def woven(lo, hi):
-            dst = hid[:, lo:hi, :].rearrange("p (c i) t -> p c t i", i=4)
-            src = picked[:, :, lo:hi].rearrange("p t (c i) -> p c t i", i=4)
-            return dst, src
-
-        dst, src = woven(0, ROUND_ON_VECTOR)
-        nc.vector.tensor_scalar_max(dst, src, 0.0)
-        dst, src = woven(ROUND_ON_VECTOR, O)
-        nc.scalar.activation(dst, src, ACT.Relu)
-
-        hq_w = sbuf("hq_w", O, U32)
-        hq_s = sbuf("hq_s", O, U8)
-        nc.vector.quantize_mx(
-            out=hq_w[:].bitcast(E5M2), scales=hq_s[:],
-            in_=hid[:].rearrange("p o t -> p (o t)"),
-        )
-
-        tz_picked = [sbuf("tz_picked%d" % h, O, F32) for h in range(N // P)]
-        for h in range(N // P):
-            nc.scalar.activation(tz_picked[h][:], tz_rows[h][:].indirect(entries[:]), ACT.Copy)
-
-        for h, queue in enumerate((nc.sync, nc.scalar)):
-            cols = slice(h * P, (h + 1) * P)
-            nc.tensor.matmul_mx(
-                out=p_ps[h][:],
-                lhsT=wb_w[:, cols].bitcast(E4M3), lhsT_scale=wb_s[:, cols],
-                rhs=hq_w[:].bitcast(E5M2), rhs_scale=hq_s[:],
-                start=False, stop=True,
+        hq_w = [sbuf("hq_w%d" % g, P, U32) for g in range(O // P)]
+        hq_s = [sbuf("hq_s%d" % g, P, U8) for g in range(O // P)]
+        for g in range(O // P):
+            nc.vector.tensor_scalar_max(
+                hid[g][:].rearrange("p (c i) t -> p c t i", i=4),
+                picked[:, :, halves[g]].rearrange("p t (c i) -> p c t i", i=4),
+                0.0,
             )
-            y = sbuf("y%d" % h, O, F32)
-            nc.vector.tensor_tensor(y[:], p_ps[h][:], tz_picked[h][:], ALU.add)
-            queue.dma_start(out[cols, :], y[:])
+            nc.vector.quantize_mx(
+                out=hq_w[g][:].bitcast(E5M2), scales=hq_s[g][:],
+                in_=hid[g][:].rearrange("p o t -> p (o t)"),
+            )
+
+        tz_picked = keep.tile([P, N * O // P], F32, name="tz_picked", tag="pg3", align_bytes=64)
+        for g in range(O // P):
+            entries_g = entries[:, g * P // 16 : (g + 1) * P // 16]
+            for h in range(N // P):
+                place = tz_picked[:, g * N + h * P : g * N + (h + 1) * P]
+                nc.scalar.activation(place, tz_rows[h][:].indirect(entries_g), ACT.Copy)
+
+        out_rows = out.rearrange("(h p) o -> p h o", p=P)
+        for g in range(O // P):
+            for h in range(N // P):
+                cols = slice(h * P, (h + 1) * P)
+                nc.tensor.matmul_mx(
+                    out=p_ps[g][:, h, :],
+                    lhsT=wb_w[:, cols].bitcast(E4M3), lhsT_scale=wb_s[:, cols],
+                    rhs=hq_w[g][:].bitcast(E5M2), rhs_scale=hq_s[g][:],
+                    start=False, stop=(h == N // P - 1),
+                )
+            y = keep.tile([P, N // P, P], F32, name="y%d" % g, align_bytes=64)
+            nc.vector.tensor_tensor(
+                y[:].rearrange("p h o -> p (h o)"), p_ps[g][:].rearrange("p h o -> p (h o)"),
+                tz_picked[:, g * N : (g + 1) * N], ALU.add,
+            )
+            nc.sync.dma_start(out_rows[:, :, halves[g]], y[:])

from contextlib import ExitStack

import concourse.mybir as mybir

K, T, J, R, C, O, N, E = 512, 1024, 256, 512, 512, 256, 256, 1024
FLOPS = 2 * K * R * J + 2 * R * N * O + 2 * K * N * O

F32 = mybir.dt.float32
BF16 = mybir.dt.bfloat16
I32 = mybir.dt.int32
U32 = mybir.dt.uint32
U16 = mybir.dt.uint16
U8 = mybir.dt.uint8
E4M3 = mybir.dt.float8_e4m3fn_x4
E5M2 = mybir.dt.float8_e5m2_x4
E2M1 = mybir.dt.float4_e2m1fn_x4
ALU = mybir.AluOpType
ACT = mybir.ActivationFunctionType

P = 128
PACK = 4
QUADS = 4
BOARDS = 3


def tile_list_postedtwice_solo_further_tabled_kernel(
    tc, xt_words, xt_scales, w_words, w_scales, wb_words, wb_scales, ws_words, ws_scales,
    tz, offs, offs2, offs3, offs4, offs5, offs6, out,
):
    nc = tc.nc

    with ExitStack() as ctx:
        keep = ctx.enter_context(tc.tile_pool(name="keep", bufs=1))
        psum = ctx.enter_context(tc.psum_pool(name="psum", bufs=1))

        def sbuf(name, width, dtype, tag=None):
            return keep.tile([P, width], dtype, name=name, tag=tag or name, align_bytes=64)

        def load_list(name, src):
            lst = keep.tile([P, J // 16], U16, name=name)
            nc.sync.dma_start(lst[:], src)
            return lst

        def load_scale_rows(queue, plane, src):
            for q in range(QUADS):
                queue.dma_start(
                    plane[32 * q : 32 * q + 4, :].bitcast(I32),
                    src[0, 4 * q : 4 * q + 4, :].bitcast(I32),
                )

        def word_rows(src):
            return src[0].rearrange("p n b -> p (n b)").bitcast(I32)

        xt_s = sbuf("xt_s", T, U8)
        w_s = sbuf("w_s", R, U8)
        wb_s = sbuf("wb_s", N, U8)
        ws_s = sbuf("ws_s", N, U8)
        xt_s_landed = sbuf("xt_s_landed", T, U8)
        for plane in (w_s, xt_s):
            nc.vector.memset(plane[:].bitcast(I32), 0)

        xt_w = sbuf("xt_w", T, U16)
        w_w = sbuf("w_w", R, U32)
        slots = load_list("slots", offs)
        load_scale_rows(nc.sync, xt_s_landed, xt_scales)
        nc.sync.dma_start(xt_w[:].bitcast(I32), xt_words[0].bitcast(I32))
        nc.sync.dma_start(w_w[:].bitcast(I32), word_rows(w_words))
        load_scale_rows(nc.sync, w_s, w_scales)
        shorts = load_list("shorts", offs5)
        posts_v = load_list("posts_v", offs3)
        posts_w = load_list("posts_w", offs2)
        reads = load_list("reads", offs4)
        entries = load_list("entries", offs6)

        pw = [sbuf("pw%d" % b, C, F32) for b in range(BOARDS - 1)]
        pv = [sbuf("pv%d" % b, C, F32) for b in range(BOARDS - 1)]
        for b, engine in enumerate((nc.vector, nc.gpsimd)):
            engine.memset(pv[b][:], 0.0)
            engine.memset(pw[b][:], 0.0)
        for plane in (ws_s, wb_s):
            nc.gpsimd.memset(plane[:].bitcast(I32), 0)

        ws_w = sbuf("ws_w", N, U32)
        wb_w = sbuf("wb_w", N, U32)
        tz_rows = [sbuf("tz_rows%d" % h, E, F32) for h in range(N // P)]
        load_scale_rows(nc.sync, ws_s, ws_scales)
        load_scale_rows(nc.sync, wb_s, wb_scales)
        nc.sync.dma_start(ws_w[:].bitcast(I32), word_rows(ws_words))
        nc.sync.dma_start(wb_w[:].bitcast(I32), word_rows(wb_words))
        for h in range(N // P):
            nc.sync.dma_start(tz_rows[h][:], tz[h * P : (h + 1) * P, :])

        for q in range(QUADS):
            live = slice(32 * q, 32 * q + 4)
            nc.vector.tensor_copy(xt_s[live, :].bitcast(I32), xt_s_landed[live, :].bitcast(I32))

        xg_w = sbuf("xg_w", J, U16)
        xg_s = sbuf("xg_s", J, U8)
        nc.vector.tensor_copy(xg_w[:], xt_w[:].indirect(slots[:]))
        nc.vector.tensor_copy(xg_s[:], xt_s[:].indirect(slots[:]))

        wd_w = sbuf("wd_w", R, U32)
        nc.scalar.copy(
            wd_w[:].rearrange("p (t m) -> p m t", t=PACK),
            w_w[:].rearrange("p (m t) -> p m t", t=PACK),
        )
        w_s_dealt = w_s[:].rearrange("p (m t) -> p t m", t=PACK)
        wd_s_first = sbuf("wd_s_first", P, U8)
        wd_s_rest = sbuf("wd_s_rest", R - P, U8)
        nc.vector.tensor_copy(wd_s_first[:], w_s_dealt[:, 0, :])
        nc.vector.tensor_copy(
            wd_s_rest[:].rearrange("p (t m) -> p t m", m=P), w_s_dealt[:, 1:, :]
        )
        wd_s = [wd_s_first[:]] + [wd_s_rest[:, t * P : (t + 1) * P] for t in range(PACK - 1)]

        xs_w = sbuf("xs_w", O, U16)
        xs_s = sbuf("xs_s", O, U8)

        a_ps0 = psum.tile([P, J], F32, name="a_ps0")
        a_ps1 = psum.tile([P, J], F32, name="a_ps1")
        a_ps23 = psum.tile([P, 2 * J], F32, name="a_ps23")
        a_ps = [a_ps0[:], a_ps1[:], a_ps23[:, :J], a_ps23[:, J:]]
        for t in range(PACK):
            nc.tensor.matmul_mx(
                out=a_ps[t],
                lhsT=wd_w[:, t * P : (t + 1) * P].bitcast(E5M2), lhsT_scale=wd_s[t],
                rhs=xg_w[:].bitcast(E2M1), rhs_scale=xg_s[:],
                start=True, stop=True,
            )

        pv.append(sbuf("pv2", C, F32, tag="wd_w"))
        pw.append(sbuf("pw2", C, F32, tag="xg_w"))
        nc.gpsimd.memset(pv[2][:], 0.0)
        nc.gpsimd.memset(pw[2][:], 0.0)

        a0 = sbuf("a0", J, F32)
        a1 = sbuf("a1", J, F32)
        a23 = sbuf("a23", 2 * J, F32)
        a = [a0[:], a1[:], a23[:, :J], a23[:, J:]]
        pg = [sbuf("pg%d" % t, C, F32) for t in range(PACK)]
        picked = keep.tile([P, PACK, O], F32, name="picked", align_bytes=64)

        def post(t):
            nc.vector.tensor_copy(pw[t % BOARDS][:].indirect(posts_w[:]), a[t])
            nc.scalar.activation(pv[t % BOARDS][:].indirect(posts_v[:]), a[t], ACT.Copy)

        def join(t, engine):
            engine.tensor_tensor(pg[t][:], pw[t % BOARDS][:], pv[t % BOARDS][:], ALU.add)

        def read(t):
            nc.scalar.activation(picked[:, t, :], pg[t][:].indirect(reads[:]), ACT.Copy)

        nc.scalar.copy(a0[:], a_ps0[:])
        nc.scalar.copy(a1[:], a_ps1[:])
        post(0)
        nc.scalar.copy(a23[:], a_ps23[:])
        post(1)
        join(0, nc.gpsimd)
        nc.vector.tensor_copy(xs_w[:], xt_w[:].indirect(shorts[:]))
        nc.vector.tensor_copy(xs_s[:], xt_s[:].indirect(shorts[:]))
        post(2)
        join(1, nc.gpsimd)
        post(3)
        join(2, nc.gpsimd)
        nc.vector.tensor_copy(picked[:, 0, :], pg[0][:].indirect(reads[:]))
        read(1)
        read(2)
        join(3, nc.vector)

        halves = [slice(g * P, (g + 1) * P) for g in range(O // P)]
        p_ps = [psum.tile([P, N // P, P], F32, name="p_ps%d" % g) for g in range(O // P)]
        for g, reads_g in enumerate(halves):
            for h in range(N // P):
                cols = slice(h * P, (h + 1) * P)
                nc.tensor.matmul_mx(
                    out=p_ps[g][:, h, :],
                    lhsT=ws_w[:, cols].bitcast(E4M3), lhsT_scale=ws_s[:, cols],
                    rhs=xs_w[:, reads_g].bitcast(E2M1), rhs_scale=xs_s[:, reads_g],
                    start=(h == 0), stop=False,
                )

        last = PACK - 1
        nc.vector.tensor_copy(picked[:, last, halves[0]], pg[last][:].indirect(reads[:, : P // 16]))
        nc.scalar.activation(picked[:, last, halves[1]], pg[last][:].indirect(reads[:, P // 16 :]), ACT.Copy)

        hid = [keep.tile([P, P, PACK], BF16, name="hid%d" % g, align_bytes=64) for g in range(O // P)]

        hq_w = [sbuf("hq_w%d" % g, P, U32) for g in range(O // P)]
        hq_s = [sbuf("hq_s%d" % g, P, U8) for g in range(O // P)]
        for g in range(O // P):
            nc.vector.tensor_scalar_max(
                hid[g][:].rearrange("p (c i) t -> p c t i", i=4),
                picked[:, :, halves[g]].rearrange("p t (c i) -> p c t i", i=4),
                0.0,
            )
            nc.vector.quantize_mx(
                out=hq_w[g][:].bitcast(E5M2), scales=hq_s[g][:],
                in_=hid[g][:].rearrange("p o t -> p (o t)"),
            )

        tz_picked = keep.tile([P, N * O // P], F32, name="tz_picked", tag="pg3", align_bytes=64)
        for g in range(O // P):
            entries_g = entries[:, g * P // 16 : (g + 1) * P // 16]
            for h in range(N // P):
                place = tz_picked[:, g * N + h * P : g * N + (h + 1) * P]
                nc.scalar.activation(place, tz_rows[h][:].indirect(entries_g), ACT.Copy)

        out_rows = out.rearrange("(h p) o -> p h o", p=P)
        for g in range(O // P):
            for h in range(N // P):
                cols = slice(h * P, (h + 1) * P)
                nc.tensor.matmul_mx(
                    out=p_ps[g][:, h, :],
                    lhsT=wb_w[:, cols].bitcast(E4M3), lhsT_scale=wb_s[:, cols],
                    rhs=hq_w[g][:].bitcast(E5M2), rhs_scale=hq_s[g][:],
                    start=False, stop=(h == N // P - 1),
                )
            y = keep.tile([P, N // P, P], F32, name="y%d" % g, align_bytes=64)
            nc.vector.tensor_tensor(
                y[:].rearrange("p h o -> p (h o)"), p_ps[g][:].rearrange("p h o -> p (h o)"),
                tz_picked[:, g * N : (g + 1) * N], ALU.add,
            )
            nc.sync.dma_start(out_rows[:, :, halves[g]], y[:])
